import numpy as np
import ml_dtypes


def mxq(x, axis, fmt="e4m3"):
    dtype, down = {"e4m3": (ml_dtypes.float8_e4m3fn, 7), "e5m2": (ml_dtypes.float8_e5m2, 14)}[fmt]
    v = np.moveaxis(np.asarray(x, np.float32).astype(ml_dtypes.bfloat16).astype(np.float64), axis, -1)
    blocks = v.reshape(v.shape[:-1] + (-1, 32))
    amax = np.abs(blocks).max(-1, keepdims=True)
    byte = np.maximum(np.where(amax > 0, np.frexp(amax)[1] - 1 + 127, 0) - down, 1)
    scale = np.exp2(byte - 127.0)
    codes = (blocks / scale).astype(np.float32).astype(dtype).astype(np.float64)
    return np.moveaxis((codes * scale).reshape(v.shape), -1, axis)


WIDE = False


def mx_kscale(k):
    if not WIDE:
        return np.ones(k)
    levels = np.array([10, -10, 5, -5, 0])
    if k % 512:
        return np.exp2(np.random.permutation(np.resize(levels, k // 32))).repeat(32)
    a = np.empty((k // 512, 16))
    for p in range(k // 512):
        a[p, :8] = np.random.permutation(np.resize(levels, 8))
        for g in range(8):
            far = levels[np.abs(levels - a[p, g]) >= 10]
            a[p, g + 8] = far[np.random.randint(len(far))]
    return np.exp2(a.ravel()).repeat(32)


def f64(x):
    return np.asarray(x).astype(np.float64)


def striped(idx):
    return np.tile(idx.reshape(-1, 16).T, (8, 1)).astype(np.uint16)


def unstriped(offs):
    return offs[:16].T.reshape(-1).astype(np.int64)


def striped8(idx):
    return np.concatenate([x.reshape(-1, 16).T for x in idx]).astype(np.uint16)


def runs(offs, k):
    lists = np.stack([offs[16 * r : 16 * r + 16].T.reshape(-1) for r in range(8)]).astype(np.int64)
    return lists[np.arange(k) % 512 // 64]


def pack_weight(w):
    k, n = w.shape
    w = f64(np.asarray(w, np.float32).astype(ml_dtypes.bfloat16)).reshape(k // 32, 32, n)
    amax = np.abs(w).max(1)
    byte = np.clip(np.where(amax > 0, np.frexp(amax)[1] - 1 + 127 - 7, 1), 1, 254)
    scaled = (w * np.exp2(127.0 - byte)[:, None, :]).reshape(k, n).astype(np.float32)
    words = np.ascontiguousarray(scaled.reshape(k // 512, 128, 4, n).transpose(0, 1, 3, 2)).astype(ml_dtypes.float8_e4m3fn).view(np.uint8)
    return words, np.ascontiguousarray(byte.astype(np.uint8).reshape(k // 512, 16, n))


def unpack_weight(words, scales):
    g, p, n, _ = words.shape
    vals = np.ascontiguousarray(words).view(ml_dtypes.float8_e4m3fn).astype(np.float64) * np.repeat(np.exp2(scales.astype(np.float64) - 127.0), 8, axis=1)[..., None]
    return vals.transpose(0, 1, 3, 2).reshape(g * 512, n)

def planes(y):
    n, m = y.shape
    v = y.astype(np.float32).astype(ml_dtypes.bfloat16).astype(np.float64).reshape(n // 32, 32, m)
    top = np.abs(v).max(1)
    byte = np.clip(np.where(top > 0, np.frexp(top)[1] - 1 + 127 - 7, 1), 1, 254)
    codes = (v * np.exp2(127.0 - byte)[:, None, :]).reshape(n, m).astype(np.float32).astype(ml_dtypes.float8_e4m3fn).view(np.uint8)
    words = codes.reshape(n // 512, 128, 4, m).transpose(0, 1, 3, 2)
    return np.ascontiguousarray(words), np.ascontiguousarray(byte.astype(np.uint8).reshape(n // 512, 16, m))


K, T, S, N, H, W, G = 512, 2048, 512, 512, 512, 256, 2048


def setup_inputs():
    n = np.random.standard_normal
    s = mx_kscale(K)[:, None]
    u = mx_kscale(H)
    packed_xT = pack_weight(n((K, T)) * s)
    packed_w1 = pack_weight(n((K, H)) / np.sqrt(K) / s)
    packed_w2 = pack_weight(n((H, N)) / np.sqrt(2 * H) / u[:, None])
    packed_w3 = pack_weight(n((K, N)) / np.sqrt(2 * K) / s)
    perm = np.stack([np.random.permutation(S) for _ in range(8)])
    return {
        "x_words": packed_xT[0],
        "x_scales": packed_xT[1],
        "w1_words": packed_w1[0],
        "w1_scales": packed_w1[1],
        "gn": (np.random.uniform(0.5, 1.5, (H, 1)) * u[:, None]).astype(np.float32),
        "w2_words": packed_w2[0],
        "w2_scales": packed_w2[1],
        "w3_words": packed_w3[0],
        "w3_scales": packed_w3[1],
        "offs": striped8(np.random.randint(0, T, (8, S))),
        "n1": striped8(perm[:, :W]),
        "n2": striped8(perm[:, W:]),
        "two": striped(np.random.permutation(T)[:S]),
        "n3": striped(np.random.randint(0, S, G)),
    }


def reference(x_words, x_scales, w1_words, w1_scales, gn, w2_words, w2_scales, w3_words, w3_scales, offs, n1, n2, two, n3):
    xq = unpack_weight(x_words, x_scales)[np.arange(K)[:, None], runs(offs, K)]
    y = unpack_weight(w1_words, w1_scales).T @ xq
    pa = y[np.arange(H)[:, None], runs(n1, H)]
    pb = y[np.arange(H)[:, None], runs(n2, H)]
    rb = np.maximum(0.5 * pa, pb)
    ra = pb - pa
    ds = np.zeros((H, S))
    ds[np.arange(H)[:, None], runs(n1, H)] = ra
    dt = ds.copy()
    dt[np.arange(H)[:, None], runs(n2, H)] = rb
    z = f64(gn) * dt
    x_two = unpack_weight(x_words, x_scales)[:, unstriped(two)]
    h = unpack_weight(w2_words, w2_scales).T @ mxq(z, 0, "e4m3") + unpack_weight(w3_words, w3_scales).T @ x_two
    ex = np.exp(h)
    mb = ex[:, unstriped(n3)]
    ms = mb.reshape(N, S, 4).sum(axis=2)
    out_0 = np.log(ms + ex) - h
    return (out_0,) + planes(out_0)

@@ -1,0 +1,244 @@
+from contextlib import ExitStack
+
+import concourse.mybir as mybir
+from concourse.masks import make_identity
+
+FLOPS = 805306368
+
+F32 = mybir.dt.float32
+BF16 = mybir.dt.bfloat16
+I32 = mybir.dt.int32
+U32 = mybir.dt.uint32
+U16 = mybir.dt.uint16
+U8 = mybir.dt.uint8
+FP8X4 = mybir.dt.float8_e4m3fn_x4
+ALU = mybir.AluOpType
+ACT = mybir.ActivationFunctionType
+
+P = 128
+PACK = 4
+T = 2048
+S = 512
+W = 256
+HALF = S // 2
+BLOCKS = S // P
+SCALAR_UNITS = (1, 3, 5, 7, 9, 11, 13, 14)
+
+
+def tile_picked_hmixliftglse_none_po_kernel(
+    tc, x_words, x_scales, w1_words, w1_scales, gn, w2_words, w2_scales, w3_words, w3_scales,
+    offs, n1, n2, two, n3, out_0, out_1, out_2,
+):
+    nc = tc.nc
+    with ExitStack() as ctx:
+        keep = ctx.enter_context(tc.tile_pool(name="keep", bufs=1))
+        ring = ctx.enter_context(tc.tile_pool(name="ring", bufs=4))
+        psum = ctx.enter_context(tc.psum_pool(name="psum", bufs=1))
+
+        def as_words(dram):
+            return dram[0].rearrange("p n t -> p (n t)").bitcast(I32)
+
+        def load_list(dram, name):
+            tile = keep.tile(list(dram.shape), U16, name=name)
+            nc.sync.dma_start(tile[:], dram)
+            return tile
+
+        def load_weight_scales(queue, tile, dram, first_row):
+            for q in range(4):
+                queue.dma_start(
+                    tile[:].bitcast(I32)[32 * q + first_row : 32 * q + first_row + 4, :],
+                    dram[0].bitcast(I32)[4 * q : 4 * q + 4, :],
+                )
+
+        def deal(engine_copy, out, in_):
+            engine_copy(out[:].rearrange("p (t m) -> p m t", t=PACK), in_[:].rearrange("p (m t) -> p m t", t=PACK))
+
+        def load_and_deal_words(dram, name):
+            raw = keep.tile([P, S], U32, name=name + "_raw", tag="w_raw")
+            nc.sync.dma_start(raw[:].bitcast(I32), as_words(dram))
+            dealt = keep.tile([P, S], U32, name=name, align_bytes=64)
+            deal(nc.scalar.copy, dealt, raw)
+            return dealt
+
+        offs_t = load_list(offs, "offs_t")
+        xs = keep.tile([P, T], U8, name="xs")
+        for e in range(2):
+            rows = x_scales[0].bitcast(I32)[e:16:2, :]
+            nc.sync.dma_start(xs[:].bitcast(I32)[e:P:2, :], rows.unsqueeze(1).to_broadcast([8, 8, T // 4]))
+        s1_raw = keep.tile([P, S], U8, name="s1_raw")
+        for q in range(4):
+            rows = w1_scales[0].bitcast(I32)[4 * q : 4 * q + 4, :]
+            queue = nc.sync if q < 2 else nc.gpsimd
+            queue.dma_start(s1_raw[:].bitcast(I32)[32 * q : 32 * q + 32, :], rows.unsqueeze(0).to_broadcast([8, 4, S // 4]))
+        xw = keep.tile([P, T], U32, name="xw")
+        nc.sync.dma_start(xw[:].bitcast(I32), as_words(x_words))
+
+        w1 = load_and_deal_words(w1_words, "w1")
+        n1_t = load_list(n1, "n1_t")
+        n2_t = load_list(n2, "n2_t")
+        two_t = load_list(two, "two_t")
+        n3_t = load_list(n3, "n3_t")
+
+        def pick_scales(list_t, name):
+            gathered = keep.tile([P, S], U8, name=name + "_gathered", tag=name + "_bytes")
+            nc.vector.tensor_copy(gathered[:], xs[:].indirect(list_t[:]))
+            placed = keep.tile([P, S], U8, name=name, align_bytes=64)
+            nc.vector.tensor_copy(placed[:].bitcast(I32), gathered[:].bitcast(I32))
+            for e in range(2):
+                nc.sync.dma_start(placed[:].bitcast(I32)[2 + e : P : 32, :], gathered[:].bitcast(I32)[16 + e : P : 32, :])
+            return placed
+
+        def pick_words(list_t, name):
+            gathered = keep.tile([P, S], U32, name=name, align_bytes=64)
+            nc.vector.tensor_copy(gathered[:], xw[:].indirect(list_t[:]))
+            return gathered
+
+        xq_s = pick_scales(offs_t, "xq_s")
+        s1 = keep.tile([P, S], U8, name="s1", align_bytes=64)
+        deal(nc.vector.tensor_copy, s1, s1_raw)
+        x2_s = pick_scales(two_t, "x2_s")
+        xq_w = pick_words(offs_t, "xq_w")
+
+        y_banks = [psum.tile([P, S], F32, name="y%d" % t, tag="a%d" % t) for t in range(PACK)]
+        for t in range(PACK):
+            cols = slice(t * P, (t + 1) * P)
+            nc.tensor.matmul_mx(
+                out=y_banks[t][:], lhsT=w1[:, cols].bitcast(FP8X4), lhsT_scale=s1[:, cols],
+                rhs=xq_w[:].bitcast(FP8X4), rhs_scale=xq_s[:], start=True, stop=True,
+            )
+        x2_w = pick_words(two_t, "x2_w")
+
+        gain = keep.tile([P, PACK], F32, name="gain")
+        nc.gpsimd.dma_start(gain[:], gn.rearrange("(p t) o -> p (t o)", t=PACK))
+        s23_raw = keep.tile([P, S], U8, name="s23_raw", tag="xq_s_bytes")
+        nc.gpsimd.memset(s23_raw[:].bitcast(I32), 0)
+        load_weight_scales(nc.sync, s23_raw, w3_scales, 0)
+        load_weight_scales(nc.sync, s23_raw, w2_scales, 4)
+        ident = keep.tile([P, P], F32, name="ident")
+        make_identity(nc, ident[:])
+
+        zb = keep.tile([P, S, PACK], BF16, name="zb", align_bytes=64)
+        y = [keep.tile([P, S], F32, name="y_sb%d" % t) for t in range(PACK)]
+        neg_pa = [keep.tile([P, W], F32, name="neg_pa%d" % t) for t in range(PACK)]
+        pb = [keep.tile([P, W], F32, name="pb%d" % t) for t in range(PACK)]
+        rb = [keep.tile([P, W], F32, name="rb%d" % t) for t in range(PACK)]
+        dt = [keep.tile([P, S], F32, name="dt%d" % t) for t in range(PACK)]
+
+        def fetch_pairs(t):
+            nc.scalar.copy(y[t][:], y_banks[t][:])
+            nc.scalar.activation(neg_pa[t][:], y[t][:].indirect(n1_t[:]), ACT.Copy, scale=-1.0)
+            if t == 0:
+                nc.vector.tensor_copy(pb[t][:], y[t][:].indirect(n2_t[:]))
+            else:
+                nc.scalar.activation(pb[t][:], y[t][:].indirect(n2_t[:]), ACT.Copy)
+
+        def larger(t):
+            nc.vector.scalar_tensor_tensor(rb[t][:], neg_pa[t][:], -0.5, pb[t][:], ALU.mult, ALU.max)
+
+        def round_z(t, cols):
+            nc.scalar.activation(zb[:, cols, t], dt[t][:, cols], ACT.Copy, scale=gain[:, t : t + 1])
+
+        fetch_pairs(0)
+        for t in range(PACK):
+            if t + 1 < PACK:
+                fetch_pairs(t + 1)
+            larger(t)
+            nc.vector.tensor_tensor(dt[t][:].indirect(n1_t[:]), pb[t][:], neg_pa[t][:], ALU.add)
+            nc.vector.tensor_copy(dt[t][:].indirect(n2_t[:]), rb[t][:])
+            if t == 0:
+                w3 = load_and_deal_words(w3_words, "w3")
+                s23 = keep.tile([P, S], U8, name="s23", align_bytes=64)
+                deal(nc.vector.tensor_copy, s23, s23_raw)
+            if t == 1:
+                w2 = load_and_deal_words(w2_words, "w2")
+            if t + 1 < PACK:
+                round_z(t, slice(0, S))
+
+        h_banks = [psum.tile([P, S], F32, name="h%d" % t, tag="b%d" % t) for t in range(PACK)]
+        for t in range(PACK):
+            cols = slice(t * P, (t + 1) * P)
+            nc.tensor.matmul_mx(
+                out=h_banks[t][:], lhsT=w3[:, cols].bitcast(FP8X4), lhsT_scale=s23[:, cols],
+                rhs=x2_w[:].bitcast(FP8X4), rhs_scale=x2_s[:], start=True, stop=False,
+            )
+
+        z_w = keep.tile([P, S], U32, name="z_w", align_bytes=64)
+        z_s = keep.tile([P, S], U8, name="z_s", align_bytes=64)
+        for half in range(2):
+            round_z(PACK - 1, slice(half * HALF, (half + 1) * HALF))
+        for half in range(2):
+            places = slice(half * HALF, (half + 1) * HALF)
+            nc.vector.quantize_mx(
+                out=z_w[:, places].bitcast(FP8X4), scales=z_s[:, places],
+                in_=zb[:, places, :].rearrange("p j t -> p (j t)"),
+            )
+            for t in range(PACK):
+                cols = slice(t * P, (t + 1) * P)
+                nc.tensor.matmul_mx(
+                    out=h_banks[t][:, places], lhsT=w2[:, cols].bitcast(FP8X4), lhsT_scale=s23[4:P, cols],
+                    rhs=z_w[:, places].bitcast(FP8X4), rhs_scale=z_s[:, places], start=False, stop=(half == 1),
+                )
+
+        ex = [keep.tile([P, S], F32, name="ex%d" % t) for t in range(PACK)]
+        h = keep.tile([P, PACK, S], F32, name="h")
+        for t in range(PACK):
+            nc.scalar.activation(ex[t][:], h_banks[t][:], ACT.Exp)
+        o_w = keep.tile([P, S], U32, name="o_w", align_bytes=64)
+        o_s = keep.tile([P, S], U8, name="o_s", align_bytes=64)
+        res = [keep.tile([P, PACK, P], F32, name="res%d" % b) for b in range(BLOCKS)]
+        out_rows = out_0.rearrange("(p t) j -> p t j", t=PACK)
+        sums = {}
+        logs = {}
+
+        def gather_and_sum(u):
+            b, t = divmod(u, PACK)
+            on_scalar = u in SCALAR_UNITS
+            members = ring.tile([P, PACK * P], F32, name="members")
+            for half in range(2):
+                entries = n3_t[:, 32 * b + 16 * half : 32 * b + 16 * half + 16]
+                if on_scalar:
+                    nc.scalar.activation(members[:, half * W : (half + 1) * W], ex[t][:].indirect(entries), ACT.Copy)
+                else:
+                    apart = members[:].rearrange("p (m j) -> p j m", m=PACK)
+                    nc.vector.tensor_copy(apart[:, half * 64 : (half + 1) * 64, :], ex[t][:].indirect(entries))
+            bank = psum.tile([P, P], F32, name="sum%d" % u, tag="a%d" % (u % PACK))
+            nc.tensor.matmul(bank[:], ex[t][:, b * P : (b + 1) * P], ident[:], is_transpose=True, start=True, stop=False)
+            for m in range(PACK):
+                member = members[:, m : PACK * P : PACK] if on_scalar else members[:, m * P : (m + 1) * P]
+                nc.tensor.matmul(bank[:], member, ident[:], is_transpose=True, start=False, stop=(m == PACK - 1))
+            sums[u] = bank
+
+        def take_log(u):
+            turned = ring.tile([P, P], F32, name="turned")
+            nc.scalar.activation(turned[:], sums[u][:], ACT.Ln)
+            bank = psum.tile([P, P], F32, name="log%d" % u, tag="b%d" % (u % PACK))
+            nc.tensor.transpose(bank[:], turned[:], ident[:])
+            logs[u] = bank
+
+        def finish(u):
+            b, t = divmod(u, PACK)
+            places = slice(b * P, (b + 1) * P)
+            nc.vector.tensor_tensor(res[b][:, t, :], logs[u][:], h[:, t, places], ALU.subtract)
+            if t == PACK - 1:
+                nc.sync.dma_start(out_rows[:, :, places], res[b][:])
+                rounded = ring.tile([P, P, PACK], BF16, name="rounded", align_bytes=64)
+                nc.vector.tensor_copy(rounded[:], res[b][:].rearrange("p t j -> p j t"))
+                nc.vector.quantize_mx(
+                    out=o_w[:, places].bitcast(FP8X4), scales=o_s[:, places],
+                    in_=rounded[:].rearrange("p j t -> p (j t)"),
+                )
+                nc.sync.dma_start(as_words(out_1)[:, places], o_w[:].bitcast(I32)[:, places])
+
+        units = BLOCKS * PACK
+        for step in range(units + 3):
+            if step < units:
+                gather_and_sum(step)
+            if step < PACK:
+                nc.vector.tensor_copy(h[:, step, :], h_banks[step][:])
+            if 2 <= step < units + 2:
+                take_log(step - 2)
+            if 3 <= step:
+                finish(step - 3)
+        for j in range(4):
+            queue = nc.sync if j % 2 == 0 else nc.scalar
+            queue.dma_start(out_2[0].bitcast(I32)[j:16:4, :], o_s[:].bitcast(I32)[j:P:32, :])

@@ -22,7 +22,14 @@ S = 512
 W = 256
 HALF = S // 2
 BLOCKS = S // P
-SCALAR_UNITS = (1, 3, 5, 7, 9, 11, 13, 14)
+SCALAR_UNITS = (3, 4, 6, 13, 14, 15)
+SCALAR_ROUNDS = (0, 1)
+MEMBER_SLOT = {}
+ROUND_SLOT = ("rounded0", "turned3", "rounded2", "rounded3")
+VECTOR_COLUMNS = 384
+DT_SLOT = ("dt0", "s_raw", "dt2", "dt3")
+RB_SLOT = ("rb0", "dt2")
+PAIRED_UNITS = (13, 14, 15)
 
 
 def tile_picked_hmixliftglse_none_po_kernel(
@@ -53,39 +60,40 @@ def tile_picked_hmixliftglse_none_po_kernel(
         def deal(engine_copy, out, in_):
             engine_copy(out[:].rearrange("p (t m) -> p m t", t=PACK), in_[:].rearrange("p (m t) -> p m t", t=PACK))
 
-        def load_and_deal_words(dram, name):
-            raw = keep.tile([P, S], U32, name=name + "_raw", tag="w_raw")
+        def load_and_deal_words(dram, name, staging):
+            raw = keep.tile([P, S], U32, name=name + "_raw", tag=staging, align_bytes=64)
             nc.sync.dma_start(raw[:].bitcast(I32), as_words(dram))
             dealt = keep.tile([P, S], U32, name=name, align_bytes=64)
             deal(nc.scalar.copy, dealt, raw)
             return dealt
 
+        ex = [keep.tile([P, 2 * S], F32, name="ex%d" % t) for t in range(PACK)]
+        for t in range(PACK):
+            nc.vector.memset(ex[t][:, S:], 0.0)
         offs_t = load_list(offs, "offs_t")
         xs = keep.tile([P, T], U8, name="xs")
-        for e in range(2):
-            rows = x_scales[0].bitcast(I32)[e:16:2, :]
-            nc.sync.dma_start(xs[:].bitcast(I32)[e:P:2, :], rows.unsqueeze(1).to_broadcast([8, 8, T // 4]))
-        s1_raw = keep.tile([P, S], U8, name="s1_raw")
+        nc.sync.dma_start(xs[:].bitcast(I32), x_scales[0].bitcast(I32).unsqueeze(1).to_broadcast([16, 8, T // 4]))
+        s1_raw = keep.tile([P, S], U8, name="s1_raw", tag="s_raw", align_bytes=64)
         for q in range(4):
             rows = w1_scales[0].bitcast(I32)[4 * q : 4 * q + 4, :]
             queue = nc.sync if q < 2 else nc.gpsimd
             queue.dma_start(s1_raw[:].bitcast(I32)[32 * q : 32 * q + 32, :], rows.unsqueeze(0).to_broadcast([8, 4, S // 4]))
+        n1_t = load_list(n1, "n1_t")
         xw = keep.tile([P, T], U32, name="xw")
         nc.sync.dma_start(xw[:].bitcast(I32), as_words(x_words))
 
-        w1 = load_and_deal_words(w1_words, "w1")
-        n1_t = load_list(n1, "n1_t")
+        w1 = load_and_deal_words(w1_words, "w1", "w_raw")
         n2_t = load_list(n2, "n2_t")
         two_t = load_list(two, "two_t")
         n3_t = load_list(n3, "n3_t")
 
         def pick_scales(list_t, name):
-            gathered = keep.tile([P, S], U8, name=name + "_gathered", tag=name + "_bytes")
+            gathered = keep.tile([P, S], U8, name=name + "_gathered", tag=name + "_bytes", align_bytes=64)
             nc.vector.tensor_copy(gathered[:], xs[:].indirect(list_t[:]))
             placed = keep.tile([P, S], U8, name=name, align_bytes=64)
             nc.vector.tensor_copy(placed[:].bitcast(I32), gathered[:].bitcast(I32))
-            for e in range(2):
-                nc.sync.dma_start(placed[:].bitcast(I32)[2 + e : P : 32, :], gathered[:].bitcast(I32)[16 + e : P : 32, :])
+            for j in range(1, 4):
+                nc.sync.dma_start(placed[:].bitcast(I32)[j:P:32, :], gathered[:].bitcast(I32)[8 * j : P : 32, :])
             return placed
 
         def pick_words(list_t, name):
@@ -99,146 +107,194 @@ def tile_picked_hmixliftglse_none_po_kernel(
         x2_s = pick_scales(two_t, "x2_s")
         xq_w = pick_words(offs_t, "xq_w")
 
-        y_banks = [psum.tile([P, S], F32, name="y%d" % t, tag="a%d" % t) for t in range(PACK)]
-        for t in range(PACK):
+        def open_banks(name, first_tags, other_tags):
+            halves = [
+                (psum.tile([P, HALF], F32, name="%s0_%d" % (name, i), tag=first_tags[i]), slice(i * HALF, (i + 1) * HALF))
+                for i in range(2)
+            ]
+            whole = [
+                [(psum.tile([P, S], F32, name="%s%d" % (name, t), tag=other_tags[t - 1]), slice(0, S))]
+                for t in range(1, PACK)
+            ]
+            return [halves] + whole
+
+        def multiply(banks, t, weights, weight_scales, words, scales, start, stop):
             cols = slice(t * P, (t + 1) * P)
-            nc.tensor.matmul_mx(
-                out=y_banks[t][:], lhsT=w1[:, cols].bitcast(FP8X4), lhsT_scale=s1[:, cols],
-                rhs=xq_w[:].bitcast(FP8X4), rhs_scale=xq_s[:], start=True, stop=True,
-            )
+            for bank, places in banks[t]:
+                nc.tensor.matmul_mx(
+                    out=bank[:], lhsT=weights[:, cols].bitcast(FP8X4), lhsT_scale=weight_scales[:, cols],
+                    rhs=words[:, places].bitcast(FP8X4), rhs_scale=scales[:, places], start=start, stop=stop,
+                )
+
+        y_banks = open_banks("y", ("a0", "b0"), ("a1", "a2", "a3"))
+        for t in (0, 2, 1, 3):
+            multiply(y_banks, t, w1, s1, xq_w, xq_s, True, True)
         x2_w = pick_words(two_t, "x2_w")
 
         gain = keep.tile([P, PACK], F32, name="gain")
         nc.gpsimd.dma_start(gain[:], gn.rearrange("(p t) o -> p (t o)", t=PACK))
-        s23_raw = keep.tile([P, S], U8, name="s23_raw", tag="xq_s_bytes")
+        s23_raw = keep.tile([P, S], U8, name="s23_raw", tag="s_raw", align_bytes=64)
         nc.gpsimd.memset(s23_raw[:].bitcast(I32), 0)
         load_weight_scales(nc.sync, s23_raw, w3_scales, 0)
         load_weight_scales(nc.sync, s23_raw, w2_scales, 4)
         ident = keep.tile([P, P], F32, name="ident")
         make_identity(nc, ident[:])
 
-        zb = keep.tile([P, S, PACK], BF16, name="zb", align_bytes=64)
-        y = [keep.tile([P, S], F32, name="y_sb%d" % t) for t in range(PACK)]
-        neg_pa = [keep.tile([P, W], F32, name="neg_pa%d" % t) for t in range(PACK)]
-        pb = [keep.tile([P, W], F32, name="pb%d" % t) for t in range(PACK)]
-        rb = [keep.tile([P, W], F32, name="rb%d" % t) for t in range(PACK)]
-        dt = [keep.tile([P, S], F32, name="dt%d" % t) for t in range(PACK)]
-
-        def fetch_pairs(t):
-            nc.scalar.copy(y[t][:], y_banks[t][:])
-            nc.scalar.activation(neg_pa[t][:], y[t][:].indirect(n1_t[:]), ACT.Copy, scale=-1.0)
-            if t == 0:
-                nc.vector.tensor_copy(pb[t][:], y[t][:].indirect(n2_t[:]))
-            else:
-                nc.scalar.activation(pb[t][:], y[t][:].indirect(n2_t[:]), ACT.Copy)
-
-        def larger(t):
-            nc.vector.scalar_tensor_tensor(rb[t][:], neg_pa[t][:], -0.5, pb[t][:], ALU.mult, ALU.max)
-
-        def round_z(t, cols):
-            nc.scalar.activation(zb[:, cols, t], dt[t][:, cols], ACT.Copy, scale=gain[:, t : t + 1])
-
-        fetch_pairs(0)
-        for t in range(PACK):
-            if t + 1 < PACK:
-                fetch_pairs(t + 1)
-            larger(t)
-            nc.vector.tensor_tensor(dt[t][:].indirect(n1_t[:]), pb[t][:], neg_pa[t][:], ALU.add)
-            nc.vector.tensor_copy(dt[t][:].indirect(n2_t[:]), rb[t][:])
-            if t == 0:
-                w3 = load_and_deal_words(w3_words, "w3")
+        neg_pa = [keep.tile([P, 2, W], F32, name="neg_pa%d" % i) for i in range(2)]
+        pb = [keep.tile([P, 2, W], F32, name="pb%d" % i) for i in range(2)]
+        for i in range(2):
+            for k in range(2):
+                y = keep.tile([P, S], F32, name="y%d" % (i + 2 * k), tag="y")
+                for bank, places in y_banks[i + 2 * k]:
+                    nc.scalar.copy(y[:, places], bank[:])
+                nc.scalar.activation(neg_pa[i][:, k, :], y[:].indirect(n1_t[:]), ACT.Copy, scale=-1.0)
+                if i + k == 0:
+                    nc.vector.tensor_copy(pb[i][:, k, :], y[:].indirect(n2_t[:]))
+                else:
+                    nc.scalar.activation(pb[i][:, k, :], y[:].indirect(n2_t[:]), ACT.Copy)
+        w3 = load_and_deal_words(w3_words, "w3", "w_raw")
+        w2 = load_and_deal_words(w2_words, "w2", "xq_s_bytes")
+        zb = keep.tile([P, S, PACK], BF16, name="zb", tag="xq_s_bytes", align_bytes=64)
+        last = PACK - 1
+        for i in range(2):
+            dt = [keep.tile([P, S], F32, name="dt%d" % (i + 2 * k), tag=DT_SLOT[i + 2 * k], align_bytes=64) for k in range(2)]
+            rb = keep.tile([P, 2, W], F32, name="rb%d" % i, tag=RB_SLOT[i], align_bytes=64)
+            nc.vector.tensor_tensor(dt[0][:].indirect(n1_t[:]), pb[i][:, 0, :], neg_pa[i][:, 0, :], ALU.add)
+            nc.vector.scalar_tensor_tensor(
+                rb[:].rearrange("p k w -> p (k w)"), neg_pa[i][:].rearrange("p k w -> p (k w)"), -0.5,
+                pb[i][:].rearrange("p k w -> p (k w)"), ALU.mult, ALU.max,
+            )
+            nc.vector.tensor_tensor(dt[1][:].indirect(n1_t[:]), pb[i][:, 1, :], neg_pa[i][:, 1, :], ALU.add)
+            for k in range(2):
+                t = i + 2 * k
+                nc.vector.tensor_copy(dt[k][:].indirect(n2_t[:]), rb[:, k, :])
+                if t < last:
+                    nc.scalar.activation(zb[:, :, t], dt[k][:], ACT.Copy, scale=gain[:, t : t + 1])
+                else:
+                    cut = VECTOR_COLUMNS
+                    nc.vector.tensor_scalar(zb[:, :cut, t], dt[k][:, :cut], gain[:, t : t + 1], None, ALU.mult)
+                    nc.scalar.activation(zb[:, cut:, t], dt[k][:, cut:], ACT.Copy, scale=gain[:, t : t + 1])
+            if i == 0:
                 s23 = keep.tile([P, S], U8, name="s23", align_bytes=64)
                 deal(nc.vector.tensor_copy, s23, s23_raw)
-            if t == 1:
-                w2 = load_and_deal_words(w2_words, "w2")
-            if t + 1 < PACK:
-                round_z(t, slice(0, S))
 
-        h_banks = [psum.tile([P, S], F32, name="h%d" % t, tag="b%d" % t) for t in range(PACK)]
+        h_banks = open_banks("h", ("a3", "b0"), ("b1", "b2", "b3"))
         for t in range(PACK):
-            cols = slice(t * P, (t + 1) * P)
-            nc.tensor.matmul_mx(
-                out=h_banks[t][:], lhsT=w3[:, cols].bitcast(FP8X4), lhsT_scale=s23[:, cols],
-                rhs=x2_w[:].bitcast(FP8X4), rhs_scale=x2_s[:], start=True, stop=False,
-            )
-
+            multiply(h_banks, t, w3, s23, x2_w, x2_s, True, False)
         z_w = keep.tile([P, S], U32, name="z_w", align_bytes=64)
         z_s = keep.tile([P, S], U8, name="z_s", align_bytes=64)
-        for half in range(2):
-            round_z(PACK - 1, slice(half * HALF, (half + 1) * HALF))
         for half in range(2):
             places = slice(half * HALF, (half + 1) * HALF)
             nc.vector.quantize_mx(
                 out=z_w[:, places].bitcast(FP8X4), scales=z_s[:, places],
                 in_=zb[:, places, :].rearrange("p j t -> p (j t)"),
             )
-            for t in range(PACK):
-                cols = slice(t * P, (t + 1) * P)
-                nc.tensor.matmul_mx(
-                    out=h_banks[t][:, places], lhsT=w2[:, cols].bitcast(FP8X4), lhsT_scale=s23[4:P, cols],
-                    rhs=z_w[:, places].bitcast(FP8X4), rhs_scale=z_s[:, places], start=False, stop=(half == 1),
-                )
+        for t in range(PACK):
+            multiply(h_banks, t, w2, s23[4:P, :], z_w, z_s, False, True)
 
-        ex = [keep.tile([P, S], F32, name="ex%d" % t) for t in range(PACK)]
         h = keep.tile([P, PACK, S], F32, name="h")
         for t in range(PACK):
-            nc.scalar.activation(ex[t][:], h_banks[t][:], ACT.Exp)
+            for bank, places in h_banks[t]:
+                nc.scalar.activation(ex[t][:, places], bank[:], ACT.Exp)
         o_w = keep.tile([P, S], U32, name="o_w", align_bytes=64)
         o_s = keep.tile([P, S], U8, name="o_s", align_bytes=64)
         res = [keep.tile([P, PACK, P], F32, name="res%d" % b) for b in range(BLOCKS)]
         out_rows = out_0.rearrange("(p t) j -> p t j", t=PACK)
         sums = {}
         logs = {}
+        groups = [[0, 1, 3, 2], [4, 5, 6, 7], [8, 9, 10, 11], [13, 12], [14], [15]]
+        sum_tags = ["a0", "a1", "a0", "a1", "a2", "a3"]
+        log_tags = ["a2", "a3", "b0", "b1", "b2", "b3"]
 
-        def gather_and_sum(u):
-            b, t = divmod(u, PACK)
-            on_scalar = u in SCALAR_UNITS
-            members = ring.tile([P, PACK * P], F32, name="members")
-            for half in range(2):
-                entries = n3_t[:, 32 * b + 16 * half : 32 * b + 16 * half + 16]
+        def gather_and_sum(g):
+            bank = psum.tile([P, P * len(groups[g])], F32, name="sum%d" % g, tag=sum_tags[g])
+            sums[g] = bank
+            for u in groups[g]:
+                i = u - min(groups[g])
+                b, t = divmod(u, PACK)
+                on_scalar = u in SCALAR_UNITS
+                members = keep.tile([P, PACK * P], F32, name="members%d" % u, tag=MEMBER_SLOT.get(u, "members%d" % u), align_bytes=64)
+                picked = ex[t][:].indirect(n3_t[:, 32 * b : 32 * (b + 1)])
                 if on_scalar:
-                    nc.scalar.activation(members[:, half * W : (half + 1) * W], ex[t][:].indirect(entries), ACT.Copy)
+                    nc.scalar.activation(members[:], picked, ACT.Copy)
                 else:
-                    apart = members[:].rearrange("p (m j) -> p j m", m=PACK)
-                    nc.vector.tensor_copy(apart[:, half * 64 : (half + 1) * 64, :], ex[t][:].indirect(entries))
-            bank = psum.tile([P, P], F32, name="sum%d" % u, tag="a%d" % (u % PACK))
-            nc.tensor.matmul(bank[:], ex[t][:, b * P : (b + 1) * P], ident[:], is_transpose=True, start=True, stop=False)
-            for m in range(PACK):
-                member = members[:, m : PACK * P : PACK] if on_scalar else members[:, m * P : (m + 1) * P]
-                nc.tensor.matmul(bank[:], member, ident[:], is_transpose=True, start=False, stop=(m == PACK - 1))
-            sums[u] = bank
+                    nc.vector.tensor_copy(members[:].rearrange("p (m j) -> p j m", m=PACK), picked)
+                if u in PAIRED_UNITS:
+                    pairs = ring.tile([P, 2 * P], F32, name="pairs")
+                    by_place = members[:].rearrange("p (j m) -> p j m", m=PACK)
+                    nc.gpsimd.tensor_tensor(
+                        pairs[:].rearrange("p (m j) -> p j m", m=2), by_place[:, :, 0:2], by_place[:, :, 2:4], ALU.add
+                    )
+                    terms = [pairs[:, m * P : (m + 1) * P] for m in range(2)]
+                elif on_scalar:
+                    terms = [members[:, m : PACK * P : PACK] for m in range(PACK)]
+                else:
+                    terms = [members[:, m * P : (m + 1) * P] for m in range(PACK)]
+                target = bank[:, i * P : (i + 1) * P]
+                nc.tensor.matmul(target, ex[t][:, b * P : (b + 1) * P], ident[:], is_transpose=True, start=True, stop=False)
+                for m, term in enumerate(terms):
+                    nc.tensor.matmul(target, term, ident[:], is_transpose=True, start=False, stop=(m == len(terms) - 1))
 
-        def take_log(u):
-            turned = ring.tile([P, P], F32, name="turned")
-            nc.scalar.activation(turned[:], sums[u][:], ACT.Ln)
-            bank = psum.tile([P, P], F32, name="log%d" % u, tag="b%d" % (u % PACK))
-            nc.tensor.transpose(bank[:], turned[:], ident[:])
-            logs[u] = bank
+        def take_log(g):
+            width = P * len(groups[g])
+            turned = keep.tile([P, width], F32, name="turned%d" % g, tag="turned%d" % g, align_bytes=64)
+            nc.scalar.activation(turned[:], sums[g][:], ACT.Ln)
+            bank = psum.tile([P, width], F32, name="log%d" % g, tag=log_tags[g])
+            for i in range(len(groups[g])):
+                nc.tensor.transpose(bank[:, i * P : (i + 1) * P], turned[:, i * P : (i + 1) * P], ident[:])
+            logs[g] = bank
 
-        def finish(u):
-            b, t = divmod(u, PACK)
+        def subtract(g):
+            b, t0 = divmod(min(groups[g]), PACK)
+            rows = slice(t0, t0 + len(groups[g]))
             places = slice(b * P, (b + 1) * P)
-            nc.vector.tensor_tensor(res[b][:, t, :], logs[u][:], h[:, t, places], ALU.subtract)
-            if t == PACK - 1:
+            nc.vector.tensor_tensor(
+                res[b][:, rows, :], logs[g][:].rearrange("p (t j) -> p t j", j=P), h[:, rows, places], ALU.subtract
+            )
+            if rows.stop == PACK:
                 nc.sync.dma_start(out_rows[:, :, places], res[b][:])
-                rounded = ring.tile([P, P, PACK], BF16, name="rounded", align_bytes=64)
-                nc.vector.tensor_copy(rounded[:], res[b][:].rearrange("p t j -> p j t"))
-                nc.vector.quantize_mx(
-                    out=o_w[:, places].bitcast(FP8X4), scales=o_s[:, places],
-                    in_=rounded[:].rearrange("p j t -> p (j t)"),
-                )
-                nc.sync.dma_start(as_words(out_1)[:, places], o_w[:].bitcast(I32)[:, places])
 
-        units = BLOCKS * PACK
-        for step in range(units + 3):
-            if step < units:
-                gather_and_sum(step)
-            if step < PACK:
-                nc.vector.tensor_copy(h[:, step, :], h_banks[step][:])
-            if 2 <= step < units + 2:
-                take_log(step - 2)
-            if 3 <= step:
-                finish(step - 3)
+        def hand_on(b):
+            places = slice(b * P, (b + 1) * P)
+            rounded = keep.tile([P, P, PACK], BF16, name="rounded%d" % b, tag=ROUND_SLOT[b], align_bytes=64)
+            by_place = res[b][:].rearrange("p t j -> p j t")
+            if b == 0:
+                nc.gpsimd.tensor_scalar(rounded[:], by_place, 1.0, 0.0, ALU.mult, ALU.add)
+            elif b == 1:
+                nc.scalar.copy(rounded[:], by_place)
+            else:
+                nc.vector.tensor_copy(rounded[:], by_place)
+            nc.vector.quantize_mx(
+                out=o_w[:, places].bitcast(FP8X4), scales=o_s[:, places],
+                in_=rounded[:].rearrange("p j t -> p (j t)"),
+            )
+
+        def keep_h(half):
+            places = slice(half * HALF, (half + 1) * HALF)
+            nc.scalar.copy(h[:, 0, places], h_banks[0][half][0][:])
+            for t in range(1, PACK):
+                nc.scalar.copy(h[:, t, places], h_banks[t][0][0][:, places])
+
+        gather_and_sum(0)
+        gather_and_sum(1)
+        take_log(0)
+        keep_h(0)
+        gather_and_sum(2)
+        take_log(1)
+        subtract(0)
+        gather_and_sum(3)
+        gather_and_sum(4)
+        subtract(1)
+        gather_and_sum(5)
+        keep_h(1)
+        for g in range(2, 6):
+            take_log(g)
+        for g in range(2, 6):
+            subtract(g)
+        for b in range(BLOCKS):
+            hand_on(b)
+        for places in (slice(0, S - P), slice(S - P, S)):
+            nc.sync.dma_start(as_words(out_1)[:, places], o_w[:].bitcast(I32)[:, places])
         for j in range(4):
             queue = nc.sync if j % 2 == 0 else nc.scalar
             queue.dma_start(out_2[0].bitcast(I32)[j:16:4, :], o_s[:].bitcast(I32)[j:P:32, :])

from contextlib import ExitStack

import concourse.mybir as mybir
from concourse.masks import make_identity

FLOPS = 805306368

F32 = mybir.dt.float32
BF16 = mybir.dt.bfloat16
I32 = mybir.dt.int32
U32 = mybir.dt.uint32
U16 = mybir.dt.uint16
U8 = mybir.dt.uint8
FP8X4 = mybir.dt.float8_e4m3fn_x4
ALU = mybir.AluOpType
ACT = mybir.ActivationFunctionType

P = 128
PACK = 4
T = 2048
S = 512
W = 256
HALF = S // 2
BLOCKS = S // P
SCALAR_UNITS = (3, 4, 6, 13, 14, 15)
SCALAR_ROUNDS = (0, 1)
MEMBER_SLOT = {}
ROUND_SLOT = ("rounded0", "turned3", "rounded2", "rounded3")
VECTOR_COLUMNS = 384
DT_SLOT = ("dt0", "s_raw", "dt2", "dt3")
RB_SLOT = ("rb0", "dt2")
PAIRED_UNITS = (13, 14, 15)


def tile_picked_hmixliftglse_none_po_kernel(
    tc, x_words, x_scales, w1_words, w1_scales, gn, w2_words, w2_scales, w3_words, w3_scales,
    offs, n1, n2, two, n3, out_0, out_1, out_2,
):
    nc = tc.nc
    with ExitStack() as ctx:
        keep = ctx.enter_context(tc.tile_pool(name="keep", bufs=1))
        ring = ctx.enter_context(tc.tile_pool(name="ring", bufs=4))
        psum = ctx.enter_context(tc.psum_pool(name="psum", bufs=1))

        def as_words(dram):
            return dram[0].rearrange("p n t -> p (n t)").bitcast(I32)

        def load_list(dram, name):
            tile = keep.tile(list(dram.shape), U16, name=name)
            nc.sync.dma_start(tile[:], dram)
            return tile

        def load_weight_scales(queue, tile, dram, first_row):
            for q in range(4):
                queue.dma_start(
                    tile[:].bitcast(I32)[32 * q + first_row : 32 * q + first_row + 4, :],
                    dram[0].bitcast(I32)[4 * q : 4 * q + 4, :],
                )

        def deal(engine_copy, out, in_):
            engine_copy(out[:].rearrange("p (t m) -> p m t", t=PACK), in_[:].rearrange("p (m t) -> p m t", t=PACK))

        def load_and_deal_words(dram, name, staging):
            raw = keep.tile([P, S], U32, name=name + "_raw", tag=staging, align_bytes=64)
            nc.sync.dma_start(raw[:].bitcast(I32), as_words(dram))
            dealt = keep.tile([P, S], U32, name=name, align_bytes=64)
            deal(nc.scalar.copy, dealt, raw)
            return dealt

        ex = [keep.tile([P, 2 * S], F32, name="ex%d" % t) for t in range(PACK)]
        for t in range(PACK):
            nc.vector.memset(ex[t][:, S:], 0.0)
        offs_t = load_list(offs, "offs_t")
        xs = keep.tile([P, T], U8, name="xs")
        nc.sync.dma_start(xs[:].bitcast(I32), x_scales[0].bitcast(I32).unsqueeze(1).to_broadcast([16, 8, T // 4]))
        s1_raw = keep.tile([P, S], U8, name="s1_raw", tag="s_raw", align_bytes=64)
        for q in range(4):
            rows = w1_scales[0].bitcast(I32)[4 * q : 4 * q + 4, :]
            queue = nc.sync if q < 2 else nc.gpsimd
            queue.dma_start(s1_raw[:].bitcast(I32)[32 * q : 32 * q + 32, :], rows.unsqueeze(0).to_broadcast([8, 4, S // 4]))
        n1_t = load_list(n1, "n1_t")
        xw = keep.tile([P, T], U32, name="xw")
        nc.sync.dma_start(xw[:].bitcast(I32), as_words(x_words))

        w1 = load_and_deal_words(w1_words, "w1", "w_raw")
        n2_t = load_list(n2, "n2_t")
        two_t = load_list(two, "two_t")
        n3_t = load_list(n3, "n3_t")

        def pick_scales(list_t, name):
            gathered = keep.tile([P, S], U8, name=name + "_gathered", tag=name + "_bytes", align_bytes=64)
            nc.vector.tensor_copy(gathered[:], xs[:].indirect(list_t[:]))
            placed = keep.tile([P, S], U8, name=name, align_bytes=64)
            nc.vector.tensor_copy(placed[:].bitcast(I32), gathered[:].bitcast(I32))
            for j in range(1, 4):
                nc.sync.dma_start(placed[:].bitcast(I32)[j:P:32, :], gathered[:].bitcast(I32)[8 * j : P : 32, :])
            return placed

        def pick_words(list_t, name):
            gathered = keep.tile([P, S], U32, name=name, align_bytes=64)
            nc.vector.tensor_copy(gathered[:], xw[:].indirect(list_t[:]))
            return gathered

        xq_s = pick_scales(offs_t, "xq_s")
        s1 = keep.tile([P, S], U8, name="s1", align_bytes=64)
        deal(nc.vector.tensor_copy, s1, s1_raw)
        x2_s = pick_scales(two_t, "x2_s")
        xq_w = pick_words(offs_t, "xq_w")

        def open_banks(name, first_tags, other_tags):
            halves = [
                (psum.tile([P, HALF], F32, name="%s0_%d" % (name, i), tag=first_tags[i]), slice(i * HALF, (i + 1) * HALF))
                for i in range(2)
            ]
            whole = [
                [(psum.tile([P, S], F32, name="%s%d" % (name, t), tag=other_tags[t - 1]), slice(0, S))]
                for t in range(1, PACK)
            ]
            return [halves] + whole

        def multiply(banks, t, weights, weight_scales, words, scales, start, stop):
            cols = slice(t * P, (t + 1) * P)
            for bank, places in banks[t]:
                nc.tensor.matmul_mx(
                    out=bank[:], lhsT=weights[:, cols].bitcast(FP8X4), lhsT_scale=weight_scales[:, cols],
                    rhs=words[:, places].bitcast(FP8X4), rhs_scale=scales[:, places], start=start, stop=stop,
                )

        y_banks = open_banks("y", ("a0", "b0"), ("a1", "a2", "a3"))
        for t in (0, 2, 1, 3):
            multiply(y_banks, t, w1, s1, xq_w, xq_s, True, True)
        x2_w = pick_words(two_t, "x2_w")

        gain = keep.tile([P, PACK], F32, name="gain")
        nc.gpsimd.dma_start(gain[:], gn.rearrange("(p t) o -> p (t o)", t=PACK))
        s23_raw = keep.tile([P, S], U8, name="s23_raw", tag="s_raw", align_bytes=64)
        nc.gpsimd.memset(s23_raw[:].bitcast(I32), 0)
        load_weight_scales(nc.sync, s23_raw, w3_scales, 0)
        load_weight_scales(nc.sync, s23_raw, w2_scales, 4)
        ident = keep.tile([P, P], F32, name="ident")
        make_identity(nc, ident[:])

        neg_pa = [keep.tile([P, 2, W], F32, name="neg_pa%d" % i) for i in range(2)]
        pb = [keep.tile([P, 2, W], F32, name="pb%d" % i) for i in range(2)]
        for i in range(2):
            for k in range(2):
                y = keep.tile([P, S], F32, name="y%d" % (i + 2 * k), tag="y")
                for bank, places in y_banks[i + 2 * k]:
                    nc.scalar.copy(y[:, places], bank[:])
                nc.scalar.activation(neg_pa[i][:, k, :], y[:].indirect(n1_t[:]), ACT.Copy, scale=-1.0)
                if i + k == 0:
                    nc.vector.tensor_copy(pb[i][:, k, :], y[:].indirect(n2_t[:]))
                else:
                    nc.scalar.activation(pb[i][:, k, :], y[:].indirect(n2_t[:]), ACT.Copy)
        w3 = load_and_deal_words(w3_words, "w3", "w_raw")
        w2 = load_and_deal_words(w2_words, "w2", "xq_s_bytes")
        zb = keep.tile([P, S, PACK], BF16, name="zb", tag="xq_s_bytes", align_bytes=64)
        last = PACK - 1
        for i in range(2):
            dt = [keep.tile([P, S], F32, name="dt%d" % (i + 2 * k), tag=DT_SLOT[i + 2 * k], align_bytes=64) for k in range(2)]
            rb = keep.tile([P, 2, W], F32, name="rb%d" % i, tag=RB_SLOT[i], align_bytes=64)
            nc.vector.tensor_tensor(dt[0][:].indirect(n1_t[:]), pb[i][:, 0, :], neg_pa[i][:, 0, :], ALU.add)
            nc.vector.scalar_tensor_tensor(
                rb[:].rearrange("p k w -> p (k w)"), neg_pa[i][:].rearrange("p k w -> p (k w)"), -0.5,
                pb[i][:].rearrange("p k w -> p (k w)"), ALU.mult, ALU.max,
            )
            nc.vector.tensor_tensor(dt[1][:].indirect(n1_t[:]), pb[i][:, 1, :], neg_pa[i][:, 1, :], ALU.add)
            for k in range(2):
                t = i + 2 * k
                nc.vector.tensor_copy(dt[k][:].indirect(n2_t[:]), rb[:, k, :])
                if t < last:
                    nc.scalar.activation(zb[:, :, t], dt[k][:], ACT.Copy, scale=gain[:, t : t + 1])
                else:
                    cut = VECTOR_COLUMNS
                    nc.vector.tensor_scalar(zb[:, :cut, t], dt[k][:, :cut], gain[:, t : t + 1], None, ALU.mult)
                    nc.scalar.activation(zb[:, cut:, t], dt[k][:, cut:], ACT.Copy, scale=gain[:, t : t + 1])
            if i == 0:
                s23 = keep.tile([P, S], U8, name="s23", align_bytes=64)
                deal(nc.vector.tensor_copy, s23, s23_raw)

        h_banks = open_banks("h", ("a3", "b0"), ("b1", "b2", "b3"))
        for t in range(PACK):
            multiply(h_banks, t, w3, s23, x2_w, x2_s, True, False)
        z_w = keep.tile([P, S], U32, name="z_w", align_bytes=64)
        z_s = keep.tile([P, S], U8, name="z_s", align_bytes=64)
        for half in range(2):
            places = slice(half * HALF, (half + 1) * HALF)
            nc.vector.quantize_mx(
                out=z_w[:, places].bitcast(FP8X4), scales=z_s[:, places],
                in_=zb[:, places, :].rearrange("p j t -> p (j t)"),
            )
        for t in range(PACK):
            multiply(h_banks, t, w2, s23[4:P, :], z_w, z_s, False, True)

        h = keep.tile([P, PACK, S], F32, name="h")
        for t in range(PACK):
            for bank, places in h_banks[t]:
                nc.scalar.activation(ex[t][:, places], bank[:], ACT.Exp)
        o_w = keep.tile([P, S], U32, name="o_w", align_bytes=64)
        o_s = keep.tile([P, S], U8, name="o_s", align_bytes=64)
        res = [keep.tile([P, PACK, P], F32, name="res%d" % b) for b in range(BLOCKS)]
        out_rows = out_0.rearrange("(p t) j -> p t j", t=PACK)
        sums = {}
        logs = {}
        groups = [[0, 1, 3, 2], [4, 5, 6, 7], [8, 9, 10, 11], [13, 12], [14], [15]]
        sum_tags = ["a0", "a1", "a0", "a1", "a2", "a3"]
        log_tags = ["a2", "a3", "b0", "b1", "b2", "b3"]

        def gather_and_sum(g):
            bank = psum.tile([P, P * len(groups[g])], F32, name="sum%d" % g, tag=sum_tags[g])
            sums[g] = bank
            for u in groups[g]:
                i = u - min(groups[g])
                b, t = divmod(u, PACK)
                on_scalar = u in SCALAR_UNITS
                members = keep.tile([P, PACK * P], F32, name="members%d" % u, tag=MEMBER_SLOT.get(u, "members%d" % u), align_bytes=64)
                picked = ex[t][:].indirect(n3_t[:, 32 * b : 32 * (b + 1)])
                if on_scalar:
                    nc.scalar.activation(members[:], picked, ACT.Copy)
                else:
                    nc.vector.tensor_copy(members[:].rearrange("p (m j) -> p j m", m=PACK), picked)
                if u in PAIRED_UNITS:
                    pairs = ring.tile([P, 2 * P], F32, name="pairs")
                    by_place = members[:].rearrange("p (j m) -> p j m", m=PACK)
                    nc.gpsimd.tensor_tensor(
                        pairs[:].rearrange("p (m j) -> p j m", m=2), by_place[:, :, 0:2], by_place[:, :, 2:4], ALU.add
                    )
                    terms = [pairs[:, m * P : (m + 1) * P] for m in range(2)]
                elif on_scalar:
                    terms = [members[:, m : PACK * P : PACK] for m in range(PACK)]
                else:
                    terms = [members[:, m * P : (m + 1) * P] for m in range(PACK)]
                target = bank[:, i * P : (i + 1) * P]
                nc.tensor.matmul(target, ex[t][:, b * P : (b + 1) * P], ident[:], is_transpose=True, start=True, stop=False)
                for m, term in enumerate(terms):
                    nc.tensor.matmul(target, term, ident[:], is_transpose=True, start=False, stop=(m == len(terms) - 1))

        def take_log(g):
            width = P * len(groups[g])
            turned = keep.tile([P, width], F32, name="turned%d" % g, tag="turned%d" % g, align_bytes=64)
            nc.scalar.activation(turned[:], sums[g][:], ACT.Ln)
            bank = psum.tile([P, width], F32, name="log%d" % g, tag=log_tags[g])
            for i in range(len(groups[g])):
                nc.tensor.transpose(bank[:, i * P : (i + 1) * P], turned[:, i * P : (i + 1) * P], ident[:])
            logs[g] = bank

        def subtract(g):
            b, t0 = divmod(min(groups[g]), PACK)
            rows = slice(t0, t0 + len(groups[g]))
            places = slice(b * P, (b + 1) * P)
            nc.vector.tensor_tensor(
                res[b][:, rows, :], logs[g][:].rearrange("p (t j) -> p t j", j=P), h[:, rows, places], ALU.subtract
            )
            if rows.stop == PACK:
                nc.sync.dma_start(out_rows[:, :, places], res[b][:])

        def hand_on(b):
            places = slice(b * P, (b + 1) * P)
            rounded = keep.tile([P, P, PACK], BF16, name="rounded%d" % b, tag=ROUND_SLOT[b], align_bytes=64)
            by_place = res[b][:].rearrange("p t j -> p j t")
            if b == 0:
                nc.gpsimd.tensor_scalar(rounded[:], by_place, 1.0, 0.0, ALU.mult, ALU.add)
            elif b == 1:
                nc.scalar.copy(rounded[:], by_place)
            else:
                nc.vector.tensor_copy(rounded[:], by_place)
            nc.vector.quantize_mx(
                out=o_w[:, places].bitcast(FP8X4), scales=o_s[:, places],
                in_=rounded[:].rearrange("p j t -> p (j t)"),
            )

        def keep_h(half):
            places = slice(half * HALF, (half + 1) * HALF)
            nc.scalar.copy(h[:, 0, places], h_banks[0][half][0][:])
            for t in range(1, PACK):
                nc.scalar.copy(h[:, t, places], h_banks[t][0][0][:, places])

        gather_and_sum(0)
        gather_and_sum(1)
        take_log(0)
        keep_h(0)
        gather_and_sum(2)
        take_log(1)
        subtract(0)
        gather_and_sum(3)
        gather_and_sum(4)
        subtract(1)
        gather_and_sum(5)
        keep_h(1)
        for g in range(2, 6):
            take_log(g)
        for g in range(2, 6):
            subtract(g)
        for b in range(BLOCKS):
            hand_on(b)
        for places in (slice(0, S - P), slice(S - P, S)):
            nc.sync.dma_start(as_words(out_1)[:, places], o_w[:].bitcast(I32)[:, places])
        for j in range(4):
            queue = nc.sync if j % 2 == 0 else nc.scalar
            queue.dma_start(out_2[0].bitcast(I32)[j:16:4, :], o_s[:].bitcast(I32)[j:P:32, :])
